import numpy as np, ml_dtypes
CORES = [65,66,69,71,193,194,197,199,321,322,325,327,449,450,453,455]
N = 16
import mx_ref
NC, G = 384, 2
C = np.float32(0.023)
CNT = [[0,0,0,0,0,0,0,0,304,0,0,0,0,0,0,80],[0,0,0,0,0,0,0,0,0,0,0,0,0,304,80,0],[0,0,0,0,0,0,304,80,0,0,0,0,0,0,0,0],[0,384,0,0,0,0,0,0,0,0,0,0,0,0,0,0],[0,0,0,0,0,0,0,0,0,0,0,0,304,80,0,0],[304,0,0,80,0,0,0,0,0,0,0,0,0,0,0,0],[0,0,80,0,0,0,0,304,0,0,0,0,0,0,0,0],[0,0,0,0,0,0,0,0,0,0,80,0,0,0,304,0],[80,0,0,0,0,0,0,0,0,0,0,0,0,0,0,304],[0,0,304,0,0,0,0,0,0,0,0,0,80,0,0,0],[0,0,0,0,0,304,0,0,0,80,0,0,0,0,0,0],[0,0,0,0,304,0,0,0,0,0,0,80,0,0,0,0],[0,0,0,0,0,80,0,0,0,0,304,0,0,0,0,0],[0,0,0,0,0,0,0,0,80,0,0,304,0,0,0,0],[0,0,0,0,0,0,80,0,0,304,0,0,0,0,0,0],[0,0,0,304,80,0,0,0,0,0,0,0,0,0,0,0]]
OFF = [[sum(c[:e]) for e in range(N + 1)] for c in CNT]
BF = ml_dtypes.bfloat16
def cut(t, i, w=512):
    return t[:, w * i:w * i + w]
def tile(rs):
    return np.stack(rs, axis=2).reshape(128, -1).astype(BF)
def layer(w, X):
    out = []
    for i in range(G):
        for t in range(len(X)):
            p = mx_ref.matmul(mx_ref.quantize(cut(w, len(X) * i + t)), X[t])
            z = p if t == 0 else z + p
        out.append(z)
    return out
def act(Z):
    return [np.maximum(s * z, 0) * C for z in Z for s in (1, -1)]
def setup_inputs(rng):
    def f(*shape):
        return mx_ref.flush((rng.standard_normal(shape, dtype=np.float32) * np.exp2(rng.integers(-2, 3, shape[:-1] + (1,)))).astype(BF))
    return {"x": f(N, 128, 4 * NC), "w1": f(N, 128, G * 512), "w2": f(N, 128, 512)}
def setup_inputs_blocks(rng):
    d = setup_inputs(rng)
    for k in ("x", "w1", "w2"): d[k] = mx_ref.spread(d[k], rng, 4)
    return d
def setup_inputs_wide(rng):
    d = setup_inputs(rng)
    for k in ("x", "w1", "w2"): d[k] = mx_ref.flush((d[k].astype(np.float32) * np.exp2(rng.integers(-8, 9, (N, 1, 1))).astype(np.float32)).astype(BF))
    return d
def setup_inputs_zeros(rng):
    d = setup_inputs(rng); v = d["x"].reshape(N, 128, -1, 4).copy()
    v[np.broadcast_to((rng.random((N, 1, v.shape[2], 1)) < 0.33), v.shape)] = 0
    d["x"] = v.reshape(d["x"].shape)
    return d
def reference(x, w1, w2):
    y = np.zeros((N, 128, NC), np.float32)
    for e in range(N):
        t = np.concatenate([x[j][:, 4 * OFF[j][e]:4 * OFF[j][e + 1]] for j in range(N)], axis=1)
        p = mx_ref.matmul(mx_ref.quantize(w2[e]), mx_ref.quantize(tile(act(layer(w1[e], [mx_ref.quantize(t)])))))
        c = 0
        for j in range(N):
            a, b = OFF[j][e], OFF[j][e + 1]
            y[j][:, a:b] = p[:, c:c + b - a]; c += b - a
    return {"y": y}

@@ -1,0 +1,266 @@
+from concourse.mybir import dt, AluOpType, ActivationFunctionType
+
+NT, MG, WIN = 384, 80, 128
+C = 0.023
+XW = MG + NT + MG
+
+SCRATCH = {
+    "xt": ("sbuf", [128, 4 * NT], "bfloat16"),
+    "wt": ("sbuf", [128, 4 * NT], "bfloat16"),
+    "xq": ("sbuf", [128, XW], "float8_e4m3fn_x4"),
+    "xs": ("sbuf", [128, XW], "uint8"),
+    "wq": ("sbuf", [128, NT], "float8_e4m3fn_x4"),
+    "ws": ("sbuf", [128, NT], "uint8"),
+    "mq": ("sbuf", [128, NT], "float8_e4m3fn_x4"),
+    "ms": ("sbuf", [128, NT], "uint8"),
+    "rq": ("sbuf", [128, NT], "float8_e4m3fn_x4"),
+    "rs": ("sbuf", [128, NT], "uint8"),
+    "hM": ("sbuf", [128, 4 * NT], "bfloat16"),
+    "hqM": ("sbuf", [128, NT], "float8_e4m3fn_x4"),
+    "hsM": ("sbuf", [128, NT], "uint8"),
+    "hS": ("sbuf", [128, 4 * WIN], "bfloat16"),
+    "hqS": ("sbuf", [128, WIN], "float8_e4m3fn_x4"),
+    "hsS": ("sbuf", [128, WIN], "uint8"),
+    "yo": ("sbuf", [128, NT], "float32"),
+    "roM": ("sbuf", [128, MG], "float32"),
+    "roS": ("sbuf", [128, MG], "float32"),
+    "rl": ("sbuf", [128, MG], "float32"),
+    "ps": ("psum", [128, 512 * 6], "float32"),
+}
+SEMAPHORES = (["lxa", "lxb", "lw", "qxa", "qxb", "qw", "sent", "m0", "m1", "m2", "r0", "r1", "r2", "tf", "tb", "ret",
+               "st", "st2"]
+              + [s + p + k for p in "MS" for k in "01" for s in ("z0", "z1", "ac", "hq", "pp")]
+              + ["cp" + p + k for p in "MS" for k in "0123"])
+
+
+def make_plan(T, topo):
+    cnt, cores = T.tables["CNT"], T.cores
+    n = len(cores)
+
+    def reach(p, q):
+        return p != q and topo.may_write(cores[p], cores[q]) and topo.may_write(cores[q], cores[p])
+
+    P = []
+    for j in range(n):
+        runs = sorted(((cnt[j][e], e, sum(cnt[j][:e])) for e in range(n) if cnt[j][e]), reverse=True)
+        P.append(dict(big=runs[0], small=runs[1] if len(runs) > 1 else None, wdst=None, fwd=None, tok=None, app=None,
+                      sec=None, late=False))
+    cols = [3 * p["big"][0] for p in P]
+    free = []
+    for e in range(n):
+        hold = sorted(((cnt[j][e], j) for j in range(n) if cnt[j][e]), reverse=True)
+        a = hold[0][1]
+        b = hold[1][1] if len(hold) > 1 else None
+        assert P[a]["big"][1] == e and a != e
+        relay = not reach(e, a)
+        if relay:
+            assert reach(e, b) and reach(b, a)
+            P[e]["wdst"], P[b]["fwd"], P[a]["late"] = (b, "r"), a, True
+        else:
+            P[e]["wdst"] = (a, "m")
+        if b is None:
+            continue
+        if relay or b == e:
+            P[b]["sec"] = ("own", "r" if relay else "w")
+            cols[b] += 3 * WIN
+        else:
+            opts = [s for s in (e, a) if reach(b, s)]
+            free.append((len(opts), e, a, b, opts))
+    for _, e, a, b, opts in sorted(free):
+        s = min(opts, key=lambda q: cols[q])
+        front = P[s]["big"][2] == 0
+        if s == a:
+            assert P[a]["big"][0] + cnt[b][e] == NT
+            P[a]["app"] = b
+            cols[a] += 3 * cnt[b][e]
+            P[b]["tok"] = (a, "f" if front else "b")
+        else:
+            assert P[e]["sec"] is None
+            P[e]["sec"] = ("for", b)
+            cols[e] += 3 * WIN
+            P[b]["tok"] = (e, "b" if front else "f")
+    for j in range(n):
+        P[j]["pad"] = cols[j] < 3 * NT
+    return P
+
+
+def rank_program(g, core, T, topo):
+    r = T.rank_of(core)
+    if r is None:
+        return
+    P = make_plan(T, topo)
+    me = P[r]
+    S = T.sem
+    u8 = dt.uint8
+    others = [d for d in T.cores if d != core and topo.may_write(core, d)]
+    cap = min(bin(topo.mask(core, d)).count("1") for d in others)
+    sent = [0]
+
+    def send(dst, out_ap, in_ap, rsem):
+        d = T.cores[dst]
+        rid, pid = topo.addr(d, core)
+        full, m, k = topo.mask(core, d), 0, 0
+        for i in range(16):
+            if (full >> i) & 1 and k < cap:
+                m, k = m | (1 << i), k + 1
+        g.remote_dma(out_ap, in_ap, rsem, S.sent, pid, rid, m)
+        sent[0] += k
+
+    sm = me["small"]
+    if sm is None or sm[2] == 0:
+        xa, xb = (0, WIN), (WIN, NT)
+    else:
+        xa, xb = (NT - WIN, NT), (0, NT - WIN)
+    if sm is not None:
+        assert xa[0] <= sm[2] and sm[2] + sm[0] <= xa[1]
+
+    def load_x(q, w, sem):
+        q.dma_start(T.xt[:, 4 * w[0]:4 * w[1]], T.x[:, 4 * w[0]:4 * w[1]]).then_inc(sem, 16)
+
+    def quant_x(w, lsem, qsem):
+        g.vector.wait_ge(lsem, 16)
+        g.vector.quantize_mx(T.xq[:, MG + w[0]:MG + w[1]], T.xs[:, MG + w[0]:MG + w[1]],
+                             T.xt[:, 4 * w[0]:4 * w[1]]).then_inc(qsem, 1)
+
+    def quant_w():
+        g.vector.wait_ge(S.lw, 32)
+        g.vector.quantize_mx(T.wq[:, 0:NT], T.ws[:, 0:NT], T.wt[:, 0:4 * NT]).then_inc(S.qw, 1)
+
+    if me["tok"]:
+        load_x(g.sync, xa, S.lxa)
+    g.scalar.dma_start(T.wt[:, 0:1024], T.w1[:, 0:1024]).then_inc(S.lw, 16)
+    g.sync.dma_start(T.wt[:, 1024:1536], T.w2[:, 0:512]).then_inc(S.lw, 16)
+    if not me["tok"]:
+        load_x(g.sync, xa, S.lxa)
+    load_x(g.scalar, xb, S.lxb)
+    if me["tok"]:
+        quant_x(xa, S.lxa, S.qxa)
+        quant_w()
+    else:
+        quant_w()
+        quant_x(xa, S.lxa, S.qxa)
+    quant_x(xb, S.lxb, S.qxb)
+
+    def margin(side, c):
+        return (MG - c, MG) if side == "f" else (MG + NT, MG + NT + c)
+
+    if me["tok"]:
+        dst, side = me["tok"]
+        a0, a1 = MG + sm[2], MG + sm[2] + sm[0]
+        d0, d1 = margin(side, sm[0])
+        g.wait_ge(S.qxa, 1)
+        send(dst, T.xq[:, d0:d1].bitcast(u8), T.xq[:, a0:a1].bitcast(u8), S["t" + side])
+        send(dst, T.xs[:, d0:d1], T.xs[:, a0:a1], S["t" + side])
+
+    def ship(dst, kind, sq, ss, waits):
+        dq, ds = (T.mq, T.ms) if kind == "m" else (T.rq, T.rs)
+        for i, (o, s_) in enumerate(((ds[:, 0:NT], ss[:, 0:NT]),
+                                     (dq[:, 0:256].bitcast(u8), sq[:, 0:256].bitcast(u8)),
+                                     (dq[:, 256:NT].bitcast(u8), sq[:, 256:NT].bitcast(u8)))):
+            if waits[i] is not None:
+                g.wait_ge(*waits[i])
+            send(dst, o, s_, S[kind + str(i)])
+
+    ship(me["wdst"][0], me["wdst"][1], T.wq, T.ws, [(S.qw, 1), None, None])
+    if me["fwd"] is not None:
+        ship(me["fwd"], "m", T.rq, T.rs, [(S.r0, cap), (S.r1, cap), (S.r2, cap)])
+
+    stores = [0]
+
+    def pipe(p, Wq, Ws, w1waits, w2waits, groups, segs, bank0):
+        h, hq, hs = T["h" + p], T["hq" + p], T["hs" + p]
+        te, ve, se = g.tensor, g.vector, g.scalar
+        base = [sum(b_ - a_ for a_, b_ in groups[:k]) for k in range(len(groups) + 1)]
+        for w in [(S.qxa, 1), (S.qxb, 1)] + w1waits:
+            te.wait_ge(*w)
+        for k, (lo, hi) in enumerate(groups):
+            n, kk = hi - lo, str(k)
+            for i in range(2):
+                b = 512 * (bank0 + 2 * k + i)
+                te.matmul_mx(T.ps[:, b:b + n], Wq[:, 128 * i:128 * i + 128], Ws[:, 128 * i:128 * i + 128],
+                             T.xq[:, lo:hi], T.xs[:, lo:hi], True, True).then_inc(S["z" + str(i) + p + kk], 1)
+            c0, c1 = 4 * base[k], 4 * base[k + 1]
+            z0 = T.ps[:, 512 * (bank0 + 2 * k):512 * (bank0 + 2 * k) + n]
+            z1 = T.ps[:, 512 * (bank0 + 2 * k + 1):512 * (bank0 + 2 * k + 1) + n]
+            ac = S["ac" + p + kk]
+            ve.wait_ge(S["z0" + p + kk], 1)
+            ve.tensor_scalar(h[:, c0 + 0:c1:4], z0, 0.0, C, AluOpType.max, AluOpType.mult).then_inc(ac, 1)
+            ve.tensor_scalar(h[:, c0 + 1:c1:4], z0, -C, 0.0, AluOpType.mult, AluOpType.max).then_inc(ac, 1)
+            se.wait_ge(S["z1" + p + kk], 1)
+            se.activation(h[:, c0 + 2:c1:4], z1, ActivationFunctionType.Relu, scale=C).then_inc(ac, 1)
+            se.activation(h[:, c0 + 3:c1:4], z1, ActivationFunctionType.Relu, scale=-C).then_inc(ac, 1)
+            ve.wait_ge(ac, 4)
+            ve.quantize_mx(hq[:, base[k]:base[k + 1]], hs[:, base[k]:base[k + 1]], h[:, c0:c1]).then_inc(S["hq" + p + kk], 1)
+        for w in w2waits:
+            te.wait_ge(*w)
+        for k, (lo, hi) in enumerate(groups):
+            b = 512 * (bank0 + 2 * k)
+            te.wait_ge(S["hq" + p + str(k)], 1)
+            te.matmul_mx(T.ps[:, b:b + hi - lo], Wq[:, 256:384], Ws[:, 256:384], hq[:, base[k]:base[k + 1]],
+                         hs[:, base[k]:base[k + 1]], True, True).then_inc(S["pp" + p + str(k)], 1)
+        for i, (k, a0, a1, dst) in enumerate(segs):
+            b = 512 * (bank0 + 2 * k) + a0 - groups[k][0]
+            src, cs = T.ps[:, b:b + a1 - a0], S["cp" + p + str(i)]
+            out = T.yo[:, a0 - MG:a1 - MG] if dst is None else T["ro" + p][:, 0:a1 - a0]
+            if k == 0:
+                se.wait_ge(S["pp" + p + "0"], 1)
+                se.activation(out, src, ActivationFunctionType.Copy).then_inc(cs, 1)
+            else:
+                ve.wait_ge(S["pp" + p + "1"], 1)
+                ve.tensor_copy(out, src).then_inc(cs, 1)
+            if dst is None:
+                g.sync.wait_ge(cs, 1)
+                g.sync.dma_start(T.y[:, a0 - MG:a1 - MG], out).then_inc(S.st, 16)
+                stores[0] += 16
+            else:
+                g.wait_ge(cs, 1)
+                send(dst, T.rl[:, 0:a1 - a0], out, S.ret)
+
+    def cut(groups, lo, hi, dst):
+        return [(k, max(lo, a_), min(hi, b_), dst) for k, (a_, b_) in enumerate(groups) if max(lo, a_) < min(hi, b_)]
+
+    def main():
+        bc, _, bo = me["big"]
+        lo, hi = MG + bo, MG + bo + bc
+        waits, segs = [(S.m0, cap), (S.m1, cap)], []
+        if me["app"] is not None:
+            side = "f" if bo == 0 else "b"
+            f0, f1 = margin(side, NT - bc)
+            groups = [(f0, f0 + WIN), (f0 + WIN, hi)] if side == "f" else [(f1 - WIN, f1), (lo, f1 - WIN)]
+            waits.append((S["t" + side], 2 * cap))
+            segs = cut(groups, f0, f1, me["app"])
+        else:
+            w0, w1 = (MG, MG + NT) if me["pad"] else (lo, hi)
+            groups = [(w0, (w0 + w1) // 2), ((w0 + w1) // 2, w1)]
+        pipe("M", T.mq, T.ms, waits, [(S.m2, cap)], groups, segs + cut(groups, lo, hi, None), 0)
+
+    def second():
+        kind, what = me["sec"]
+        if kind == "own":
+            groups = [(MG + xa[0], MG + xa[1])]
+            segs = cut(groups, MG + sm[2], MG + sm[2] + sm[0], None)
+            if what == "r":
+                pipe("S", T.rq, T.rs, [(S.r0, cap), (S.r1, cap)], [(S.r2, cap)], groups, segs, 4)
+            else:
+                pipe("S", T.wq, T.ws, [(S.qw, 1)], [], groups, segs, 4)
+        else:
+            side = P[what]["tok"][1]
+            f0, f1 = margin(side, P[what]["small"][0])
+            groups = [(f0, f0 + WIN)] if side == "f" else [(f1 - WIN, f1)]
+            pipe("S", T.wq, T.ws, [(S.qw, 1), (S["t" + side], 2 * cap)], [], groups, cut(groups, f0, f1, what), 4)
+
+    if me["sec"] is None:
+        main()
+    elif me["sec"] == ("own", "r") and not me["late"]:
+        main()
+        second()
+    else:
+        second()
+        main()
+
+    if me["tok"]:
+        g.scalar.wait_ge(S.ret, cap)
+        g.scalar.dma_start(T.y[:, sm[2]:sm[2] + sm[0]], T.rl[:, 0:sm[0]]).then_inc(S.st2, 16)
+        g.scalar.wait_ge(S.st2, 16)
+    g.sync.wait_ge(S.st, stores[0])
+    g.wait_ge(S.sent, sent[0])

@@ -3,6 +3,7 @@ from concourse.mybir import dt, AluOpType, ActivationFunctionType
 NT, MG, WIN = 384, 80, 128
 C = 0.023
 XW = MG + NT + MG
+WORLD = 512
 
 SCRATCH = {
     "xt": ("sbuf", [128, 4 * NT], "bfloat16"),
@@ -31,9 +32,86 @@ SEMAPHORES = (["lxa", "lxb", "lw", "qxa", "qxb", "qw", "sent", "m0", "m1", "m2",
                "st", "st2"]
               + [s + p + k for p in "MS" for k in "01" for s in ("z0", "z1", "ac", "hq", "pp")]
               + ["cp" + p + k for p in "MS" for k in "0123"])
+_PLAN = {}
+
+
+def eng(topo, cap, s, d, part=None):
+    full = topo.mask(s, d)
+    bits = [i for i in range(16) if (full >> i) & 1][:cap]
+    if part is not None:
+        bits = bits[part::2]
+    return sum(1 << i for i in bits), len(bits)
+
+
+def links(topo, ranks, s, d):
+    if not topo.may_write(s, d):
+        return None
+    hs, hd, me = topo.host(s), topo.host(d), ("eng", s)
+    if hs == hd and topo.chip(s) == topo.chip(d):
+        return [me]
+    if topo.rack(hs) != topo.rack(hd):
+        return [me, ("cable", s)] if topo.chip(s) == topo.chip(d) and s in ranks else None
+    out = ("out", hs, topo.chip(s), topo.die(s))
+    if topo.same_plane(s, d):
+        return [me, out, ("in", hd, topo.chip(d), topo.die(s))]
+    if topo.mates(s, d):
+        return [me, ("mate",) + out]
+    return [me, ("mate",) + out, ("mate out",) + out, ("in", hd, topo.chip(d), topo.die(s))]
+
+
+def routes(T, topo, flows):
+    cores = T.cores
+    near = [c for c in range(WORLD) if any(topo.host(c) == topo.host(q) and (topo.chip(c) == topo.chip(q) or topo.mates(c, q))
+                                           for q in cores)]
+    opts = []
+    for e, a, b in flows:
+        s, d, o, seen = cores[e], cores[a], [], {}
+        L = links(topo, cores, s, d)
+        if L is not None:
+            o.append((None, L))
+        if L is None or len(L) > 1:
+            for h in near:
+                if h in (s, d) or (h in cores and (b is None or h != cores[b])):
+                    continue
+                L1, L2 = links(topo, cores, s, h), links(topo, cores, h, d)
+                if L1 is None or L2 is None:
+                    continue
+                sig = tuple(l for l in L1 + L2 if l != ("eng", h))
+                seen[sig] = seen.get(sig, 0) + 1
+                if seen[sig] <= 2:
+                    o.append((h, L1 + L2))
+        opts.append(o)
+    n = len(flows)
+    order = sorted(range(n), key=lambda i: len(opts[i]))
+    low = [min(len(L) + 0.1 * (h is not None) for h, L in opts[i]) for i in order] + [0]
+    for k in range(n - 1, -1, -1):
+        low[k] += low[k + 1]
+    best, load, ch = [1e9, None], {}, {}
+
+    def dfs(k, c):
+        if c + low[k] >= best[0] - 1e-9:
+            return
+        if k == n:
+            best[0], best[1] = c, dict(ch)
+            return
+        i = order[k]
+        sc = sorted((0.1 * (h is not None) + sum(3 * load.get(l, 0) * (load.get(l, 0) + 1) + 1 for l in L), ci)
+                    for ci, (h, L) in enumerate(opts[i]))
+        for dc, ci in sc:
+            for l in opts[i][ci][1]:
+                load[l] = load.get(l, 0) + 1
+            ch[i] = ci
+            dfs(k + 1, c + dc)
+            for l in opts[i][ci][1]:
+                load[l] -= 1
+
+    dfs(0, 0.0)
+    return [opts[i][best[1][i]][0] for i in range(n)]
 
 
 def make_plan(T, topo):
+    if "P" in _PLAN:
+        return _PLAN["P"]
     cnt, cores = T.tables["CNT"], T.cores
     n = len(cores)
 
@@ -43,31 +121,38 @@ def make_plan(T, topo):
     P = []
     for j in range(n):
         runs = sorted(((cnt[j][e], e, sum(cnt[j][:e])) for e in range(n) if cnt[j][e]), reverse=True)
-        P.append(dict(big=runs[0], small=runs[1] if len(runs) > 1 else None, wdst=None, fwd=None, tok=None, app=None,
+        P.append(dict(big=runs[0], small=runs[1] if len(runs) > 1 else None, fwd=None, tok=None, app=None,
                       sec=None, late=False))
-    cols = [3 * p["big"][0] for p in P]
-    free = []
+    flows = []
     for e in range(n):
         hold = sorted(((cnt[j][e], j) for j in range(n) if cnt[j][e]), reverse=True)
-        a = hold[0][1]
-        b = hold[1][1] if len(hold) > 1 else None
-        assert P[a]["big"][1] == e and a != e
-        relay = not reach(e, a)
-        if relay:
-            assert reach(e, b) and reach(b, a)
-            P[e]["wdst"], P[b]["fwd"], P[a]["late"] = (b, "r"), a, True
-        else:
-            P[e]["wdst"] = (a, "m")
+        assert P[hold[0][1]]["big"][1] == e and hold[0][1] != e
+        flows.append((e, hold[0][1], hold[1][1] if len(hold) > 1 else None))
+    via = routes(T, topo, flows)
+    cols = [3 * p["big"][0] for p in P]
+    free, idle = [], {}
+    for e, a, b in flows:
+        if via[e] is not None:
+            P[a]["late"] = True
+            if via[e] in cores:
+                P[b]["fwd"] = e
+            else:
+                assert via[e] not in idle
+                idle[via[e]] = e
+    for e, a, b in flows:
         if b is None:
             continue
-        if relay or b == e:
-            P[b]["sec"] = ("own", "r" if relay else "w")
+        if b == e or via[e] == cores[b]:
+            P[b]["sec"] = ("own", "w" if b == e else "r")
             cols[b] += 3 * WIN
         else:
-            opts = [s for s in (e, a) if reach(b, s)]
-            free.append((len(opts), e, a, b, opts))
-    for _, e, a, b, opts in sorted(free):
-        s = min(opts, key=lambda q: cols[q])
+            free.append((e, a, b))
+    todo = []
+    for e, a, b in free:
+        opts = [s for s in (e, a) if reach(b, s) and not (s == e and P[e]["sec"] is not None)]
+        todo.append((len(opts), e, a, b, opts))
+    for _, e, a, b, opts in sorted(todo):
+        s = min(opts, key=lambda q: (q == a and P[a]["late"], cols[q]))
         front = P[s]["big"][2] == 0
         if s == a:
             assert P[a]["big"][0] + cnt[b][e] == NT
@@ -81,30 +166,55 @@ def make_plan(T, topo):
             P[b]["tok"] = (e, "b" if front else "f")
     for j in range(n):
         P[j]["pad"] = cols[j] < 3 * NT
-    return P
+    cap = min(bin(topo.mask(p, q)).count("1") for p in cores for q in cores if p != q and topo.may_write(p, q))
+    hop = {}
+    for e, a, b in flows:
+        p0 = 0 if P[e]["fwd"] is not None else None
+        if via[e] is None:
+            hop[e] = [(cores[e], cores[a], p0)]
+        else:
+            hop[e] = [(cores[e], via[e], p0), (via[e], cores[a], 1 if via[e] in cores else None)]
+    _PLAN["P"] = (P, idle, hop, cap)
+    return _PLAN["P"]
 
 
 def rank_program(g, core, T, topo):
     r = T.rank_of(core)
-    if r is None:
+    P, idle, hop, cap = make_plan(T, topo)
+    if r is None and core not in idle:
         return
-    P = make_plan(T, topo)
-    me = P[r]
     S = T.sem
     u8 = dt.uint8
-    others = [d for d in T.cores if d != core and topo.may_write(core, d)]
-    cap = min(bin(topo.mask(core, d)).count("1") for d in others)
     sent = [0]
 
-    def send(dst, out_ap, in_ap, rsem):
-        d = T.cores[dst]
+    def send(d, out_ap, in_ap, rsem, part=None):
         rid, pid = topo.addr(d, core)
-        full, m, k = topo.mask(core, d), 0, 0
-        for i in range(16):
-            if (full >> i) & 1 and k < cap:
-                m, k = m | (1 << i), k + 1
+        m, k = eng(topo, cap, core, d, part)
         g.remote_dma(out_ap, in_ap, rsem, S.sent, pid, rid, m)
         sent[0] += k
+
+    def ship(h, kind, sq, ss, waits):
+        _, d, part = h
+        dq, ds = (T.mq, T.ms) if kind == "m" else (T.rq, T.rs)
+        for i, (o, s_) in enumerate(((ds[:, 0:NT], ss[:, 0:NT]),
+                                     (dq[:, 0:256].bitcast(u8), sq[:, 0:256].bitcast(u8)),
+                                     (dq[:, 256:NT].bitcast(u8), sq[:, 256:NT].bitcast(u8)))):
+            if waits[i] is not None:
+                g.wait_ge(*waits[i])
+            send(d, o, s_, S[kind + str(i)], part)
+
+    def count(h):
+        return eng(topo, cap, *h)[1]
+
+    def forward(e):
+        k = count(hop[e][0])
+        ship(hop[e][1], "m", T.rq, T.rs, [(S.r0, k), (S.r1, k), (S.r2, k)])
+
+    if r is None:
+        forward(idle[core])
+        g.wait_ge(S.sent, sent[0])
+        return
+    me = P[r]
 
     sm = me["small"]
     if sm is None or sm[2] == 0:
@@ -149,21 +259,12 @@ def rank_program(g, core, T, topo):
         a0, a1 = MG + sm[2], MG + sm[2] + sm[0]
         d0, d1 = margin(side, sm[0])
         g.wait_ge(S.qxa, 1)
-        send(dst, T.xq[:, d0:d1].bitcast(u8), T.xq[:, a0:a1].bitcast(u8), S["t" + side])
-        send(dst, T.xs[:, d0:d1], T.xs[:, a0:a1], S["t" + side])
+        send(T.cores[dst], T.xq[:, d0:d1].bitcast(u8), T.xq[:, a0:a1].bitcast(u8), S["t" + side])
+        send(T.cores[dst], T.xs[:, d0:d1], T.xs[:, a0:a1], S["t" + side])
 
-    def ship(dst, kind, sq, ss, waits):
-        dq, ds = (T.mq, T.ms) if kind == "m" else (T.rq, T.rs)
-        for i, (o, s_) in enumerate(((ds[:, 0:NT], ss[:, 0:NT]),
-                                     (dq[:, 0:256].bitcast(u8), sq[:, 0:256].bitcast(u8)),
-                                     (dq[:, 256:NT].bitcast(u8), sq[:, 256:NT].bitcast(u8)))):
-            if waits[i] is not None:
-                g.wait_ge(*waits[i])
-            send(dst, o, s_, S[kind + str(i)])
-
-    ship(me["wdst"][0], me["wdst"][1], T.wq, T.ws, [(S.qw, 1), None, None])
+    ship(hop[r][0], "m" if len(hop[r]) == 1 else "r", T.wq, T.ws, [(S.qw, 1), None, None])
     if me["fwd"] is not None:
-        ship(me["fwd"], "m", T.rq, T.rs, [(S.r0, cap), (S.r1, cap), (S.r2, cap)])
+        forward(me["fwd"])
 
     stores = [0]
 
@@ -214,15 +315,16 @@ def rank_program(g, core, T, topo):
                 stores[0] += 16
             else:
                 g.wait_ge(cs, 1)
-                send(dst, T.rl[:, 0:a1 - a0], out, S.ret)
+                send(T.cores[dst], T.rl[:, 0:a1 - a0], out, S.ret)
 
     def cut(groups, lo, hi, dst):
         return [(k, max(lo, a_), min(hi, b_), dst) for k, (a_, b_) in enumerate(groups) if max(lo, a_) < min(hi, b_)]
 
     def main():
-        bc, _, bo = me["big"]
+        bc, be, bo = me["big"]
         lo, hi = MG + bo, MG + bo + bc
-        waits, segs = [(S.m0, cap), (S.m1, cap)], []
+        km = count(hop[be][-1])
+        waits, segs = [(S.m0, km), (S.m1, km)], []
         if me["app"] is not None:
             side = "f" if bo == 0 else "b"
             f0, f1 = margin(side, NT - bc)
@@ -232,7 +334,7 @@ def rank_program(g, core, T, topo):
         else:
             w0, w1 = (MG, MG + NT) if me["pad"] else (lo, hi)
             groups = [(w0, (w0 + w1) // 2), ((w0 + w1) // 2, w1)]
-        pipe("M", T.mq, T.ms, waits, [(S.m2, cap)], groups, segs + cut(groups, lo, hi, None), 0)
+        pipe("M", T.mq, T.ms, waits, [(S.m2, km)], groups, segs + cut(groups, lo, hi, None), 0)
 
     def second():
         kind, what = me["sec"]
@@ -240,7 +342,8 @@ def rank_program(g, core, T, topo):
             groups = [(MG + xa[0], MG + xa[1])]
             segs = cut(groups, MG + sm[2], MG + sm[2] + sm[0], None)
             if what == "r":
-                pipe("S", T.rq, T.rs, [(S.r0, cap), (S.r1, cap)], [(S.r2, cap)], groups, segs, 4)
+                kr = count(hop[me["fwd"]][0])
+                pipe("S", T.rq, T.rs, [(S.r0, kr), (S.r1, kr)], [(S.r2, kr)], groups, segs, 4)
             else:
                 pipe("S", T.wq, T.ws, [(S.qw, 1)], [], groups, segs, 4)
         else:

from concourse.mybir import dt, AluOpType, ActivationFunctionType

NT, MG, WIN = 384, 80, 128
C = 0.023
XW = MG + NT + MG
WORLD = 512

SCRATCH = {
    "xt": ("sbuf", [128, 4 * NT], "bfloat16"),
    "wt": ("sbuf", [128, 4 * NT], "bfloat16"),
    "xq": ("sbuf", [128, XW], "float8_e4m3fn_x4"),
    "xs": ("sbuf", [128, XW], "uint8"),
    "wq": ("sbuf", [128, NT], "float8_e4m3fn_x4"),
    "ws": ("sbuf", [128, NT], "uint8"),
    "mq": ("sbuf", [128, NT], "float8_e4m3fn_x4"),
    "ms": ("sbuf", [128, NT], "uint8"),
    "rq": ("sbuf", [128, NT], "float8_e4m3fn_x4"),
    "rs": ("sbuf", [128, NT], "uint8"),
    "hM": ("sbuf", [128, 4 * NT], "bfloat16"),
    "hqM": ("sbuf", [128, NT], "float8_e4m3fn_x4"),
    "hsM": ("sbuf", [128, NT], "uint8"),
    "hS": ("sbuf", [128, 4 * WIN], "bfloat16"),
    "hqS": ("sbuf", [128, WIN], "float8_e4m3fn_x4"),
    "hsS": ("sbuf", [128, WIN], "uint8"),
    "yo": ("sbuf", [128, NT], "float32"),
    "roM": ("sbuf", [128, MG], "float32"),
    "roS": ("sbuf", [128, MG], "float32"),
    "rl": ("sbuf", [128, MG], "float32"),
    "ps": ("psum", [128, 512 * 6], "float32"),
}
SEMAPHORES = (["lxa", "lxb", "lw", "qxa", "qxb", "qw", "sent", "m0", "m1", "m2", "r0", "r1", "r2", "tf", "tb", "ret",
               "st", "st2"]
              + [s + p + k for p in "MS" for k in "01" for s in ("z0", "z1", "ac", "hq", "pp")]
              + ["cp" + p + k for p in "MS" for k in "0123"])
_PLAN = {}


def eng(topo, cap, s, d, part=None):
    full = topo.mask(s, d)
    bits = [i for i in range(16) if (full >> i) & 1][:cap]
    if part is not None:
        bits = bits[part::2]
    return sum(1 << i for i in bits), len(bits)


def links(topo, ranks, s, d):
    if not topo.may_write(s, d):
        return None
    hs, hd, me = topo.host(s), topo.host(d), ("eng", s)
    if hs == hd and topo.chip(s) == topo.chip(d):
        return [me]
    if topo.rack(hs) != topo.rack(hd):
        return [me, ("cable", s)] if topo.chip(s) == topo.chip(d) and s in ranks else None
    out = ("out", hs, topo.chip(s), topo.die(s))
    if topo.same_plane(s, d):
        return [me, out, ("in", hd, topo.chip(d), topo.die(s))]
    if topo.mates(s, d):
        return [me, ("mate",) + out]
    return [me, ("mate",) + out, ("mate out",) + out, ("in", hd, topo.chip(d), topo.die(s))]


def routes(T, topo, flows):
    cores = T.cores
    near = [c for c in range(WORLD) if any(topo.host(c) == topo.host(q) and (topo.chip(c) == topo.chip(q) or topo.mates(c, q))
                                           for q in cores)]
    opts = []
    for e, a, b in flows:
        s, d, o, seen = cores[e], cores[a], [], {}
        L = links(topo, cores, s, d)
        if L is not None:
            o.append((None, L))
        if L is None or len(L) > 1:
            for h in near:
                if h in (s, d) or (h in cores and (b is None or h != cores[b])):
                    continue
                L1, L2 = links(topo, cores, s, h), links(topo, cores, h, d)
                if L1 is None or L2 is None:
                    continue
                sig = tuple(l for l in L1 + L2 if l != ("eng", h))
                seen[sig] = seen.get(sig, 0) + 1
                if seen[sig] <= 2:
                    o.append((h, L1 + L2))
        opts.append(o)
    n = len(flows)
    order = sorted(range(n), key=lambda i: len(opts[i]))
    low = [min(len(L) + 0.1 * (h is not None) for h, L in opts[i]) for i in order] + [0]
    for k in range(n - 1, -1, -1):
        low[k] += low[k + 1]
    best, load, ch = [1e9, None], {}, {}

    def dfs(k, c):
        if c + low[k] >= best[0] - 1e-9:
            return
        if k == n:
            best[0], best[1] = c, dict(ch)
            return
        i = order[k]
        sc = sorted((0.1 * (h is not None) + sum(3 * load.get(l, 0) * (load.get(l, 0) + 1) + 1 for l in L), ci)
                    for ci, (h, L) in enumerate(opts[i]))
        for dc, ci in sc:
            for l in opts[i][ci][1]:
                load[l] = load.get(l, 0) + 1
            ch[i] = ci
            dfs(k + 1, c + dc)
            for l in opts[i][ci][1]:
                load[l] -= 1

    dfs(0, 0.0)
    return [opts[i][best[1][i]][0] for i in range(n)]


def make_plan(T, topo):
    if "P" in _PLAN:
        return _PLAN["P"]
    cnt, cores = T.tables["CNT"], T.cores
    n = len(cores)

    def reach(p, q):
        return p != q and topo.may_write(cores[p], cores[q]) and topo.may_write(cores[q], cores[p])

    P = []
    for j in range(n):
        runs = sorted(((cnt[j][e], e, sum(cnt[j][:e])) for e in range(n) if cnt[j][e]), reverse=True)
        P.append(dict(big=runs[0], small=runs[1] if len(runs) > 1 else None, fwd=None, tok=None, app=None,
                      sec=None, late=False))
    flows = []
    for e in range(n):
        hold = sorted(((cnt[j][e], j) for j in range(n) if cnt[j][e]), reverse=True)
        assert P[hold[0][1]]["big"][1] == e and hold[0][1] != e
        flows.append((e, hold[0][1], hold[1][1] if len(hold) > 1 else None))
    via = routes(T, topo, flows)
    cols = [3 * p["big"][0] for p in P]
    free, idle = [], {}
    for e, a, b in flows:
        if via[e] is not None:
            P[a]["late"] = True
            if via[e] in cores:
                P[b]["fwd"] = e
            else:
                assert via[e] not in idle
                idle[via[e]] = e
    for e, a, b in flows:
        if b is None:
            continue
        if b == e or via[e] == cores[b]:
            P[b]["sec"] = ("own", "w" if b == e else "r")
            cols[b] += 3 * WIN
        else:
            free.append((e, a, b))
    todo = []
    for e, a, b in free:
        opts = [s for s in (e, a) if reach(b, s) and not (s == e and P[e]["sec"] is not None)]
        todo.append((len(opts), e, a, b, opts))
    for _, e, a, b, opts in sorted(todo):
        s = min(opts, key=lambda q: (q == a and P[a]["late"], cols[q]))
        front = P[s]["big"][2] == 0
        if s == a:
            assert P[a]["big"][0] + cnt[b][e] == NT
            P[a]["app"] = b
            cols[a] += 3 * cnt[b][e]
            P[b]["tok"] = (a, "f" if front else "b")
        else:
            assert P[e]["sec"] is None
            P[e]["sec"] = ("for", b)
            cols[e] += 3 * WIN
            P[b]["tok"] = (e, "b" if front else "f")
    for j in range(n):
        P[j]["pad"] = cols[j] < 3 * NT
    cap = min(bin(topo.mask(p, q)).count("1") for p in cores for q in cores if p != q and topo.may_write(p, q))
    hop = {}
    for e, a, b in flows:
        p0 = 0 if P[e]["fwd"] is not None else None
        if via[e] is None:
            hop[e] = [(cores[e], cores[a], p0)]
        else:
            hop[e] = [(cores[e], via[e], p0), (via[e], cores[a], 1 if via[e] in cores else None)]
    _PLAN["P"] = (P, idle, hop, cap)
    return _PLAN["P"]


def rank_program(g, core, T, topo):
    r = T.rank_of(core)
    P, idle, hop, cap = make_plan(T, topo)
    if r is None and core not in idle:
        return
    S = T.sem
    u8 = dt.uint8
    sent = [0]

    def send(d, out_ap, in_ap, rsem, part=None):
        rid, pid = topo.addr(d, core)
        m, k = eng(topo, cap, core, d, part)
        g.remote_dma(out_ap, in_ap, rsem, S.sent, pid, rid, m)
        sent[0] += k

    def ship(h, kind, sq, ss, waits):
        _, d, part = h
        dq, ds = (T.mq, T.ms) if kind == "m" else (T.rq, T.rs)
        for i, (o, s_) in enumerate(((ds[:, 0:NT], ss[:, 0:NT]),
                                     (dq[:, 0:256].bitcast(u8), sq[:, 0:256].bitcast(u8)),
                                     (dq[:, 256:NT].bitcast(u8), sq[:, 256:NT].bitcast(u8)))):
            if waits[i] is not None:
                g.wait_ge(*waits[i])
            send(d, o, s_, S[kind + str(i)], part)

    def count(h):
        return eng(topo, cap, *h)[1]

    def forward(e):
        k = count(hop[e][0])
        ship(hop[e][1], "m", T.rq, T.rs, [(S.r0, k), (S.r1, k), (S.r2, k)])

    if r is None:
        forward(idle[core])
        g.wait_ge(S.sent, sent[0])
        return
    me = P[r]

    sm = me["small"]
    if sm is None or sm[2] == 0:
        xa, xb = (0, WIN), (WIN, NT)
    else:
        xa, xb = (NT - WIN, NT), (0, NT - WIN)
    if sm is not None:
        assert xa[0] <= sm[2] and sm[2] + sm[0] <= xa[1]

    def load_x(q, w, sem):
        q.dma_start(T.xt[:, 4 * w[0]:4 * w[1]], T.x[:, 4 * w[0]:4 * w[1]]).then_inc(sem, 16)

    def quant_x(w, lsem, qsem):
        g.vector.wait_ge(lsem, 16)
        g.vector.quantize_mx(T.xq[:, MG + w[0]:MG + w[1]], T.xs[:, MG + w[0]:MG + w[1]],
                             T.xt[:, 4 * w[0]:4 * w[1]]).then_inc(qsem, 1)

    def quant_w():
        g.vector.wait_ge(S.lw, 32)
        g.vector.quantize_mx(T.wq[:, 0:NT], T.ws[:, 0:NT], T.wt[:, 0:4 * NT]).then_inc(S.qw, 1)

    if me["tok"]:
        load_x(g.sync, xa, S.lxa)
    g.scalar.dma_start(T.wt[:, 0:1024], T.w1[:, 0:1024]).then_inc(S.lw, 16)
    g.sync.dma_start(T.wt[:, 1024:1536], T.w2[:, 0:512]).then_inc(S.lw, 16)
    if not me["tok"]:
        load_x(g.sync, xa, S.lxa)
    load_x(g.scalar, xb, S.lxb)
    if me["tok"]:
        quant_x(xa, S.lxa, S.qxa)
        quant_w()
    else:
        quant_w()
        quant_x(xa, S.lxa, S.qxa)
    quant_x(xb, S.lxb, S.qxb)

    def margin(side, c):
        return (MG - c, MG) if side == "f" else (MG + NT, MG + NT + c)

    if me["tok"]:
        dst, side = me["tok"]
        a0, a1 = MG + sm[2], MG + sm[2] + sm[0]
        d0, d1 = margin(side, sm[0])
        g.wait_ge(S.qxa, 1)
        send(T.cores[dst], T.xq[:, d0:d1].bitcast(u8), T.xq[:, a0:a1].bitcast(u8), S["t" + side])
        send(T.cores[dst], T.xs[:, d0:d1], T.xs[:, a0:a1], S["t" + side])

    ship(hop[r][0], "m" if len(hop[r]) == 1 else "r", T.wq, T.ws, [(S.qw, 1), None, None])
    if me["fwd"] is not None:
        forward(me["fwd"])

    stores = [0]

    def pipe(p, Wq, Ws, w1waits, w2waits, groups, segs, bank0):
        h, hq, hs = T["h" + p], T["hq" + p], T["hs" + p]
        te, ve, se = g.tensor, g.vector, g.scalar
        base = [sum(b_ - a_ for a_, b_ in groups[:k]) for k in range(len(groups) + 1)]
        for w in [(S.qxa, 1), (S.qxb, 1)] + w1waits:
            te.wait_ge(*w)
        for k, (lo, hi) in enumerate(groups):
            n, kk = hi - lo, str(k)
            for i in range(2):
                b = 512 * (bank0 + 2 * k + i)
                te.matmul_mx(T.ps[:, b:b + n], Wq[:, 128 * i:128 * i + 128], Ws[:, 128 * i:128 * i + 128],
                             T.xq[:, lo:hi], T.xs[:, lo:hi], True, True).then_inc(S["z" + str(i) + p + kk], 1)
            c0, c1 = 4 * base[k], 4 * base[k + 1]
            z0 = T.ps[:, 512 * (bank0 + 2 * k):512 * (bank0 + 2 * k) + n]
            z1 = T.ps[:, 512 * (bank0 + 2 * k + 1):512 * (bank0 + 2 * k + 1) + n]
            ac = S["ac" + p + kk]
            ve.wait_ge(S["z0" + p + kk], 1)
            ve.tensor_scalar(h[:, c0 + 0:c1:4], z0, 0.0, C, AluOpType.max, AluOpType.mult).then_inc(ac, 1)
            ve.tensor_scalar(h[:, c0 + 1:c1:4], z0, -C, 0.0, AluOpType.mult, AluOpType.max).then_inc(ac, 1)
            se.wait_ge(S["z1" + p + kk], 1)
            se.activation(h[:, c0 + 2:c1:4], z1, ActivationFunctionType.Relu, scale=C).then_inc(ac, 1)
            se.activation(h[:, c0 + 3:c1:4], z1, ActivationFunctionType.Relu, scale=-C).then_inc(ac, 1)
            ve.wait_ge(ac, 4)
            ve.quantize_mx(hq[:, base[k]:base[k + 1]], hs[:, base[k]:base[k + 1]], h[:, c0:c1]).then_inc(S["hq" + p + kk], 1)
        for w in w2waits:
            te.wait_ge(*w)
        for k, (lo, hi) in enumerate(groups):
            b = 512 * (bank0 + 2 * k)
            te.wait_ge(S["hq" + p + str(k)], 1)
            te.matmul_mx(T.ps[:, b:b + hi - lo], Wq[:, 256:384], Ws[:, 256:384], hq[:, base[k]:base[k + 1]],
                         hs[:, base[k]:base[k + 1]], True, True).then_inc(S["pp" + p + str(k)], 1)
        for i, (k, a0, a1, dst) in enumerate(segs):
            b = 512 * (bank0 + 2 * k) + a0 - groups[k][0]
            src, cs = T.ps[:, b:b + a1 - a0], S["cp" + p + str(i)]
            out = T.yo[:, a0 - MG:a1 - MG] if dst is None else T["ro" + p][:, 0:a1 - a0]
            if k == 0:
                se.wait_ge(S["pp" + p + "0"], 1)
                se.activation(out, src, ActivationFunctionType.Copy).then_inc(cs, 1)
            else:
                ve.wait_ge(S["pp" + p + "1"], 1)
                ve.tensor_copy(out, src).then_inc(cs, 1)
            if dst is None:
                g.sync.wait_ge(cs, 1)
                g.sync.dma_start(T.y[:, a0 - MG:a1 - MG], out).then_inc(S.st, 16)
                stores[0] += 16
            else:
                g.wait_ge(cs, 1)
                send(T.cores[dst], T.rl[:, 0:a1 - a0], out, S.ret)

    def cut(groups, lo, hi, dst):
        return [(k, max(lo, a_), min(hi, b_), dst) for k, (a_, b_) in enumerate(groups) if max(lo, a_) < min(hi, b_)]

    def main():
        bc, be, bo = me["big"]
        lo, hi = MG + bo, MG + bo + bc
        km = count(hop[be][-1])
        waits, segs = [(S.m0, km), (S.m1, km)], []
        if me["app"] is not None:
            side = "f" if bo == 0 else "b"
            f0, f1 = margin(side, NT - bc)
            groups = [(f0, f0 + WIN), (f0 + WIN, hi)] if side == "f" else [(f1 - WIN, f1), (lo, f1 - WIN)]
            waits.append((S["t" + side], 2 * cap))
            segs = cut(groups, f0, f1, me["app"])
        else:
            w0, w1 = (MG, MG + NT) if me["pad"] else (lo, hi)
            groups = [(w0, (w0 + w1) // 2), ((w0 + w1) // 2, w1)]
        pipe("M", T.mq, T.ms, waits, [(S.m2, km)], groups, segs + cut(groups, lo, hi, None), 0)

    def second():
        kind, what = me["sec"]
        if kind == "own":
            groups = [(MG + xa[0], MG + xa[1])]
            segs = cut(groups, MG + sm[2], MG + sm[2] + sm[0], None)
            if what == "r":
                kr = count(hop[me["fwd"]][0])
                pipe("S", T.rq, T.rs, [(S.r0, kr), (S.r1, kr)], [(S.r2, kr)], groups, segs, 4)
            else:
                pipe("S", T.wq, T.ws, [(S.qw, 1)], [], groups, segs, 4)
        else:
            side = P[what]["tok"][1]
            f0, f1 = margin(side, P[what]["small"][0])
            groups = [(f0, f0 + WIN)] if side == "f" else [(f1 - WIN, f1)]
            pipe("S", T.wq, T.ws, [(S.qw, 1), (S["t" + side], 2 * cap)], [], groups, cut(groups, f0, f1, what), 4)

    if me["sec"] is None:
        main()
    elif me["sec"] == ("own", "r") and not me["late"]:
        main()
        second()
    else:
        second()
        main()

    if me["tok"]:
        g.scalar.wait_ge(S.ret, cap)
        g.scalar.dma_start(T.y[:, sm[2]:sm[2] + sm[0]], T.rl[:, 0:sm[0]]).then_inc(S.st2, 16)
        g.scalar.wait_ge(S.st2, 16)
    g.sync.wait_ge(S.st, stores[0])
    g.wait_ge(S.sent, sent[0])
